import numpy as np
import ml_dtypes

BF16 = ml_dtypes.bfloat16


def bf(x):
    return np.asarray(x, np.float32).astype(BF16)


def f32(x):
    return np.asarray(x, np.float32)


def f64(x):
    return np.asarray(x).astype(np.float64)


def striped(idx):
    return np.tile(idx.reshape(-1, 16).T, (8, 1))


S, K, M, N, V, D = 512, 128, 128, 1024, 16, 64


def setup_inputs():
    return {"table": bf(np.random.standard_normal((K, S))), "w": bf(2.0 * np.random.standard_normal((K, M)) / np.sqrt(K)), "offs": striped(np.random.permutation(np.tile(np.arange(S), 2))[:N])}


def reference(table, w, offs):
    idx = offs[:16].T.reshape(-1)
    x = f64(table)[:, idx]
    u = (f64(w).T @ x).reshape(M, V, D)
    u = u - u.max(axis=2, keepdims=True)
    return (u - np.log(np.exp(u).sum(axis=2, keepdims=True))).reshape(M, N)

@@ -1,0 +1,58 @@
+import concourse.mybir as mybir
+
+FLOPS = 2 * 128 * 128 * 1024
+
+BF16, F32, U16 = mybir.dt.bfloat16, mybir.dt.float32, mybir.dt.uint16
+ALU, ACT, AXIS = mybir.AluOpType, mybir.ActivationFunctionType, mybir.AxisListType
+
+SLATE = 64
+PIECE = 256
+PER_COLUMN = 16
+
+
+def tile_rows_slate_logp_rep_kernel(tc, table, w, offs, out):
+    nc = tc.nc
+    features, items = table.shape
+    states, entries = out.shape
+    pieces, slates, per_piece = entries // PIECE, entries // SLATE, PIECE // SLATE
+
+    with (
+        tc.tile_pool(name="held", bufs=1) as held,
+        tc.tile_pool(name="work", bufs=pieces) as work,
+        tc.psum_pool(name="psum", bufs=pieces) as psum,
+    ):
+        offsets = held.tile([features, entries // PER_COLUMN], U16)
+        store = held.tile([features, items], BF16)
+        weights = held.tile([features, states], BF16)
+        nc.sync.dma_start(store[:], table)
+        nc.sync.dma_start(offsets[:], offs)
+        nc.scalar.dma_start(weights[:], w)
+
+        neg_max = held.tile([states, slates], F32)
+        sums = held.tile([states, slates], F32)
+        scores = []
+        for p in range(pieces):
+            bank = psum.tile([states, per_piece, SLATE], F32)
+            scores.append(bank)
+            columns = slice(p * PIECE // PER_COLUMN, (p + 1) * PIECE // PER_COLUMN)
+            nc.tensor.matmul(bank[:].rearrange("m v t -> m (v t)"), weights[:], store[:].indirect(offsets[:, columns]),
+                             start=True, stop=True)
+            first = p * per_piece
+            nc.vector.tensor_reduce(neg_max[:, first:first + per_piece], bank[:], AXIS.X, ALU.max, negate=True)
+            exps = work.tile([states, per_piece, SLATE], F32)
+            for v in range(per_piece):
+                slate = slice(first + v, first + v + 1)
+                nc.scalar.activation(exps[:, v, :], bank[:, v, :], ACT.Exp, bias=neg_max[:, slate],
+                                     accum_out=sums[:, slate])
+
+        log_sums = held.tile([states, slates], F32)
+        nc.scalar.activation(log_sums[:], sums[:], ACT.Ln)
+        log_norm = held.tile([states, slates], F32)
+        nc.vector.tensor_tensor(log_norm[:], log_sums[:], neg_max[:], ALU.subtract)
+
+        for p in range(pieces):
+            first = p * per_piece
+            result = work.tile([states, per_piece, SLATE], F32)
+            norm = log_norm[:, first:first + per_piece].unsqueeze(2).to_broadcast([states, per_piece, SLATE])
+            nc.vector.tensor_tensor(result[:], scores[p][:], norm, ALU.subtract)
+            nc.sync.dma_start(out[:, p * PIECE:(p + 1) * PIECE], result[:].rearrange("m v t -> m (v t)"))

@@ -1,25 +1,36 @@
+import math
+
 import concourse.mybir as mybir
 
 FLOPS = 2 * 128 * 128 * 1024
 
-BF16, F32, U16 = mybir.dt.bfloat16, mybir.dt.float32, mybir.dt.uint16
+BF16, F32 = mybir.dt.bfloat16, mybir.dt.float32
+U16, U32 = mybir.dt.uint16, mybir.dt.uint32
 ALU, ACT, AXIS = mybir.AluOpType, mybir.ActivationFunctionType, mybir.AxisListType
 
 SLATE = 64
-PIECE = 256
 PER_COLUMN = 16
+HALF = 8
+SHORT = 3
+LONG = HALF - SHORT
+
+LN2 = math.log(2.0)
+GAP = LN2 - 1.0 - math.log(LN2)
+GUESS_SCALE = LN2 / 2 ** 23
+GUESS_BIAS = GAP / 2 - 127 * LN2
+STEPS = 6
 
 
 def tile_rows_slate_logp_rep_kernel(tc, table, w, offs, out):
     nc = tc.nc
     features, items = table.shape
     states, entries = out.shape
-    pieces, slates, per_piece = entries // PIECE, entries // SLATE, PIECE // SLATE
 
     with (
         tc.tile_pool(name="held", bufs=1) as held,
-        tc.tile_pool(name="work", bufs=pieces) as work,
-        tc.psum_pool(name="psum", bufs=pieces) as psum,
+        tc.tile_pool(name="halves", bufs=2) as halves,
+        tc.tile_pool(name="work", bufs=4) as work,
+        tc.psum_pool(name="psum", bufs=4) as psum,
     ):
         offsets = held.tile([features, entries // PER_COLUMN], U16)
         store = held.tile([features, items], BF16)
@@ -28,31 +39,72 @@ def tile_rows_slate_logp_rep_kernel(tc, table, w, offs, out):
         nc.sync.dma_start(offsets[:], offs)
         nc.scalar.dma_start(weights[:], w)
 
-        neg_max = held.tile([states, slates], F32)
-        sums = held.tile([states, slates], F32)
-        scores = []
-        for p in range(pieces):
-            bank = psum.tile([states, per_piece, SLATE], F32)
-            scores.append(bank)
-            columns = slice(p * PIECE // PER_COLUMN, (p + 1) * PIECE // PER_COLUMN)
-            nc.tensor.matmul(bank[:].rearrange("m v t -> m (v t)"), weights[:], store[:].indirect(offsets[:, columns]),
-                             start=True, stop=True)
-            first = p * per_piece
-            nc.vector.tensor_reduce(neg_max[:, first:first + per_piece], bank[:], AXIS.X, ALU.max, negate=True)
-            exps = work.tile([states, per_piece, SLATE], F32)
-            for v in range(per_piece):
-                slate = slice(first + v, first + v + 1)
-                nc.scalar.activation(exps[:, v, :], bank[:, v, :], ACT.Exp, bias=neg_max[:, slate],
-                                     accum_out=sums[:, slate])
+        exp_bias = held.tile([states, 1], F32)
+        nc.vector.memset(exp_bias[:], -GUESS_BIAS)
+        series_bias = held.tile([states, 1], F32)
+        nc.vector.memset(series_bias[:], 1.5 - GUESS_BIAS)
 
-        log_sums = held.tile([states, slates], F32)
-        nc.scalar.activation(log_sums[:], sums[:], ACT.Ln)
-        log_norm = held.tile([states, slates], F32)
-        nc.vector.tensor_tensor(log_norm[:], log_sums[:], neg_max[:], ALU.subtract)
+        def score(half, widths):
+            factors = halves.tile([states, HALF, STEPS], F32)
+            terms = halves.tile([states, HALF, STEPS], F32)
+            nc.vector.memset(factors[:, :, 0], 0.0)
+            nc.vector.memset(factors[:, :, 5], 1.0)
+            nc.vector.memset(terms[:, :, 0], 0.5)
+            nc.vector.memset(terms[:, :, 1:4:2], 0.0)
+            nc.vector.memset(terms[:, :, 2], -2.0)
+            banks, first = [], 0
+            for width in widths:
+                bank = psum.tile([states, width, SLATE], F32)
+                start = (half * HALF + first) * SLATE // PER_COLUMN
+                picks = offsets[:, start:start + width * SLATE // PER_COLUMN]
+                nc.tensor.matmul(bank[:].rearrange("m v t -> m (v t)"), weights[:], store[:].indirect(picks),
+                                 start=True, stop=True)
+                nc.vector.tensor_reduce(terms[:, first:first + width, 5], bank[:], AXIS.X, ALU.max, negate=True)
+                banks.append(bank)
+                first += width
+            return banks, factors, terms
 
-        for p in range(pieces):
-            first = p * per_piece
-            result = work.tile([states, per_piece, SLATE], F32)
-            norm = log_norm[:, first:first + per_piece].unsqueeze(2).to_broadcast([states, per_piece, SLATE])
-            nc.vector.tensor_tensor(result[:], scores[p][:], norm, ALU.subtract)
-            nc.sync.dma_start(out[:, p * PIECE:(p + 1) * PIECE], result[:].rearrange("m v t -> m (v t)"))
+        def normalise(banks, factors, terms):
+            sums, neg_max = factors[:, :, 1], terms[:, :, 5]
+            slate = 0
+            for bank in banks:
+                exps = work.tile(bank.shape, F32)
+                for v in range(bank.shape[1]):
+                    nc.scalar.activation(exps[:, v, :], bank[:, v, :], ACT.Exp, bias=neg_max[:, slate:slate + 1],
+                                         accum_out=sums[:, slate:slate + 1])
+                    slate += 1
+            bits = sums.bitcast(U32)
+            nc.scalar.activation(factors[:, :, 2:5:2], bits.unsqueeze(2).to_broadcast([states, HALF, 2]), ACT.Exp,
+                                 bias=exp_bias[:], scale=-GUESS_SCALE)
+            nc.scalar.activation(terms[:, :, 4], bits, ACT.Identity, bias=series_bias[:], scale=-GUESS_SCALE)
+            nc.vector.tensor_copy(factors[:, :, 3], sums)
+            scan = halves.tile([states, HALF, STEPS], F32)
+            nc.vector.tensor_tensor_scan(scan[:].rearrange("m v s -> m (v s)"),
+                                         factors[:].rearrange("m v s -> m (v s)"),
+                                         terms[:].rearrange("m v s -> m (v s)"), 0.0, ALU.mult, ALU.add)
+            return scan[:, :, STEPS - 1]
+
+        def finish_on_vector(bank, neg_norm, first_slate):
+            width = bank.shape[1]
+            result = work.tile([states, width, SLATE], F32)
+            nc.vector.tensor_tensor(result[:], bank[:], neg_norm.unsqueeze(2).to_broadcast([states, width, SLATE]),
+                                    ALU.add)
+            nc.sync.dma_start(out[:, first_slate * SLATE:(first_slate + width) * SLATE],
+                              result[:].rearrange("m v t -> m (v t)"))
+
+        def finish_on_scalar(bank, neg_norm, first_slate):
+            width = bank.shape[1]
+            result = work.tile([states, width, SLATE], F32)
+            for v in range(width):
+                nc.scalar.activation(result[:, v, :], bank[:, v, :], ACT.Identity, bias=neg_norm[:, v:v + 1])
+            nc.scalar.dma_start(out[:, first_slate * SLATE:(first_slate + width) * SLATE],
+                                result[:].rearrange("m v t -> m (v t)"))
+
+        early = score(0, (SHORT, LONG))
+        late = score(1, (LONG, SHORT))
+        early_norm = normalise(*early)
+        late_norm = normalise(*late)
+        finish_on_vector(early[0][0], early_norm[:, :SHORT], 0)
+        finish_on_vector(early[0][1], early_norm[:, SHORT:], SHORT)
+        finish_on_vector(late[0][0], late_norm[:, :LONG], HALF)
+        finish_on_scalar(late[0][1], late_norm[:, LONG:], HALF + LONG)

import math

import concourse.mybir as mybir

FLOPS = 2 * 128 * 128 * 1024

BF16, F32 = mybir.dt.bfloat16, mybir.dt.float32
U16, U32 = mybir.dt.uint16, mybir.dt.uint32
ALU, ACT, AXIS = mybir.AluOpType, mybir.ActivationFunctionType, mybir.AxisListType

SLATE = 64
PER_COLUMN = 16
HALF = 8
SHORT = 3
LONG = HALF - SHORT

LN2 = math.log(2.0)
GAP = LN2 - 1.0 - math.log(LN2)
GUESS_SCALE = LN2 / 2 ** 23
GUESS_BIAS = GAP / 2 - 127 * LN2
STEPS = 6


def tile_rows_slate_logp_rep_kernel(tc, table, w, offs, out):
    nc = tc.nc
    features, items = table.shape
    states, entries = out.shape

    with (
        tc.tile_pool(name="held", bufs=1) as held,
        tc.tile_pool(name="halves", bufs=2) as halves,
        tc.tile_pool(name="work", bufs=4) as work,
        tc.psum_pool(name="psum", bufs=4) as psum,
    ):
        offsets = held.tile([features, entries // PER_COLUMN], U16)
        store = held.tile([features, items], BF16)
        weights = held.tile([features, states], BF16)
        nc.sync.dma_start(store[:], table)
        nc.sync.dma_start(offsets[:], offs)
        nc.scalar.dma_start(weights[:], w)

        exp_bias = held.tile([states, 1], F32)
        nc.vector.memset(exp_bias[:], -GUESS_BIAS)
        series_bias = held.tile([states, 1], F32)
        nc.vector.memset(series_bias[:], 1.5 - GUESS_BIAS)

        def score(half, widths):
            factors = halves.tile([states, HALF, STEPS], F32)
            terms = halves.tile([states, HALF, STEPS], F32)
            nc.vector.memset(factors[:, :, 0], 0.0)
            nc.vector.memset(factors[:, :, 5], 1.0)
            nc.vector.memset(terms[:, :, 0], 0.5)
            nc.vector.memset(terms[:, :, 1:4:2], 0.0)
            nc.vector.memset(terms[:, :, 2], -2.0)
            banks, first = [], 0
            for width in widths:
                bank = psum.tile([states, width, SLATE], F32)
                start = (half * HALF + first) * SLATE // PER_COLUMN
                picks = offsets[:, start:start + width * SLATE // PER_COLUMN]
                nc.tensor.matmul(bank[:].rearrange("m v t -> m (v t)"), weights[:], store[:].indirect(picks),
                                 start=True, stop=True)
                nc.vector.tensor_reduce(terms[:, first:first + width, 5], bank[:], AXIS.X, ALU.max, negate=True)
                banks.append(bank)
                first += width
            return banks, factors, terms

        def normalise(banks, factors, terms):
            sums, neg_max = factors[:, :, 1], terms[:, :, 5]
            slate = 0
            for bank in banks:
                exps = work.tile(bank.shape, F32)
                for v in range(bank.shape[1]):
                    nc.scalar.activation(exps[:, v, :], bank[:, v, :], ACT.Exp, bias=neg_max[:, slate:slate + 1],
                                         accum_out=sums[:, slate:slate + 1])
                    slate += 1
            bits = sums.bitcast(U32)
            nc.scalar.activation(factors[:, :, 2:5:2], bits.unsqueeze(2).to_broadcast([states, HALF, 2]), ACT.Exp,
                                 bias=exp_bias[:], scale=-GUESS_SCALE)
            nc.scalar.activation(terms[:, :, 4], bits, ACT.Identity, bias=series_bias[:], scale=-GUESS_SCALE)
            nc.vector.tensor_copy(factors[:, :, 3], sums)
            scan = halves.tile([states, HALF, STEPS], F32)
            nc.vector.tensor_tensor_scan(scan[:].rearrange("m v s -> m (v s)"),
                                         factors[:].rearrange("m v s -> m (v s)"),
                                         terms[:].rearrange("m v s -> m (v s)"), 0.0, ALU.mult, ALU.add)
            return scan[:, :, STEPS - 1]

        def finish_on_vector(bank, neg_norm, first_slate):
            width = bank.shape[1]
            result = work.tile([states, width, SLATE], F32)
            nc.vector.tensor_tensor(result[:], bank[:], neg_norm.unsqueeze(2).to_broadcast([states, width, SLATE]),
                                    ALU.add)
            nc.sync.dma_start(out[:, first_slate * SLATE:(first_slate + width) * SLATE],
                              result[:].rearrange("m v t -> m (v t)"))

        def finish_on_scalar(bank, neg_norm, first_slate):
            width = bank.shape[1]
            result = work.tile([states, width, SLATE], F32)
            for v in range(width):
                nc.scalar.activation(result[:, v, :], bank[:, v, :], ACT.Identity, bias=neg_norm[:, v:v + 1])
            nc.scalar.dma_start(out[:, first_slate * SLATE:(first_slate + width) * SLATE],
                                result[:].rearrange("m v t -> m (v t)"))

        early = score(0, (SHORT, LONG))
        late = score(1, (LONG, SHORT))
        early_norm = normalise(*early)
        late_norm = normalise(*late)
        finish_on_vector(early[0][0], early_norm[:, :SHORT], 0)
        finish_on_vector(early[0][1], early_norm[:, SHORT:], SHORT)
        finish_on_vector(late[0][0], late_norm[:, :LONG], HALF)
        finish_on_scalar(late[0][1], late_norm[:, LONG:], HALF + LONG)
